import numpy as np
import ml_dtypes


def mxq(x, axis, fmt="e4m3"):
    dtype, down = {"e4m3": (ml_dtypes.float8_e4m3fn, 7), "e5m2": (ml_dtypes.float8_e5m2, 14)}[fmt]
    v = np.moveaxis(np.asarray(x, np.float32).astype(ml_dtypes.bfloat16).astype(np.float64), axis, -1)
    blocks = v.reshape(v.shape[:-1] + (-1, 32))
    amax = np.abs(blocks).max(-1, keepdims=True)
    byte = np.maximum(np.where(amax > 0, np.frexp(amax)[1] - 1 + 127, 0) - down, 1)
    scale = np.exp2(byte - 127.0)
    codes = (blocks / scale).astype(np.float32).astype(dtype).astype(np.float64)
    return np.moveaxis((codes * scale).reshape(v.shape), -1, axis)


WIDE = False


def mx_kscale(k):
    if not WIDE:
        return np.ones(k)
    levels = np.array([30, -30])
    if k % 512:
        return np.exp2(np.random.permutation(np.resize(levels, k // 32))).repeat(32)
    a = np.empty((k // 512, 16))
    for p in range(k // 512):
        a[p, :8] = np.random.permutation(np.resize(levels, 8))
        for g in range(8):
            far = levels[np.abs(levels - a[p, g]) >= 10]
            a[p, g + 8] = far[np.random.randint(len(far))]
    return np.exp2(a.ravel()).repeat(32)


def f64(x):
    return np.asarray(x).astype(np.float64)


def striped(idx):
    return np.tile(np.asarray(idx).reshape(-1, 16).T, (8, 1)).astype(np.uint16)


def unstriped(offs):
    return offs[:16].T.reshape(-1).astype(np.int64)


def striped8(idx):
    return np.asarray(idx).reshape(8, -1, 16).transpose(0, 2, 1).reshape(128, -1).astype(np.uint16)


def unstriped8(offs):
    return offs.reshape(8, 16, -1).transpose(0, 2, 1).reshape(8, -1).astype(np.int64)


def pick8(x, idx, run):
    r = np.arange(len(x))
    return x[r[:, None], idx[r % (8 * run) // run]]


E2M1 = np.array([0.0, 0.5, 1.0, 1.5, 2.0, 3.0, 4.0, 6.0, -0.0, -0.5, -1.0, -1.5, -2.0, -3.0, -4.0, -6.0])


def pack_weight(w, fmt):
    k, n = w.shape
    w = f64(np.asarray(w, np.float32).astype(ml_dtypes.bfloat16)).reshape(k // 32, 32, n)
    amax = np.abs(w).max(1)
    if fmt in ("e4m3", "e5m2"):
        byte = np.frexp(amax)[1] - 1 + 127 - (7 if fmt == "e4m3" else 14)
    else:
        mant, ex = np.frexp(amax / 6.0)
        byte = np.where(mant > 0.5, ex, ex - 1) + 127
    byte = np.clip(np.where(amax > 0, byte, 1), 1, 254)
    scaled = (w * np.exp2(127.0 - byte)[:, None, :]).reshape(k, n).astype(np.float32)
    by_word = np.ascontiguousarray(scaled.reshape(k // 512, 128, 4, n).transpose(0, 1, 3, 2))
    if fmt in ("e4m3", "e5m2"):
        words = by_word.astype(ml_dtypes.float8_e4m3fn if fmt == "e4m3" else ml_dtypes.float8_e5m2).view(np.uint8)
    else:
        c = by_word.astype(ml_dtypes.float4_e2m1fn).view(np.uint8) & 0xF
        words = (c[..., 0::2] | (c[..., 1::2] << 4)).reshape(k // 512, 128, 2 * n)
    return np.ascontiguousarray(words), np.ascontiguousarray(byte.astype(np.uint8).reshape(k // 512, 16, n))


def unpack_weight(words, scales, fmt):
    g, _, n = scales.shape
    words = np.ascontiguousarray(words).reshape(g, 128, n, -1)
    if fmt in ("e4m3", "e5m2"):
        vals = words.view(ml_dtypes.float8_e4m3fn if fmt == "e4m3" else ml_dtypes.float8_e5m2).astype(np.float64)
    else:
        nib = np.empty((g, 128, n, 4), np.uint8)
        nib[..., 0::2] = words & 0xF
        nib[..., 1::2] = words >> 4
        vals = E2M1[nib]
    vals = vals * np.repeat(np.exp2(scales.astype(np.float64) - 127.0), 8, axis=1)[..., None]
    return vals.transpose(0, 1, 3, 2).reshape(g * 512, n)


K, T, J, R, F, Z, M, Q, O, D, N, U = 512, 1024, 256, 512, 512, 1024, 512, 128, 128, 256, 256, 128


def setup_inputs():
    n = np.random.standard_normal
    idx = np.random.permutation(T)[:J]
    idx2 = np.random.permutation(Z)[:J]
    idx3 = np.stack([np.random.permutation(J)[:O] for _ in range(8)])
    idx4 = np.stack([np.random.permutation(J)[:O] for _ in range(8)])
    idx5 = np.random.permutation(T)[:D]
    idx6 = np.random.permutation(D)[:U]
    idx7 = np.random.permutation(D)[:U]
    fk = mx_kscale(K)
    ff = mx_kscale(F)
    fm = mx_kscale(M)
    fr = mx_kscale(R)
    xtp = pack_weight(n((K, T)) / fk[:, None], "e4m3")
    xop = pack_weight(n((F, Z)) / ff[:, None], "e2m1")
    wp = pack_weight(n((K, R)) * 1 / np.sqrt(K) * fk[:, None], "e2m1")
    w0p = pack_weight(n((F, R)) * 1 / np.sqrt(F) * ff[:, None], "e5m2")
    xcp = pack_weight(n((M, Q)) / fm[:, None], "e4m3")
    wgp = pack_weight(n((M, R)) * 1 / np.sqrt(M) * fm[:, None] * fr, "e2m1")
    wbp = pack_weight(n((R, N)) * 1 / np.sqrt(R) / fr[:, None], "e5m2")
    wsp = pack_weight(n((K, N)) * 1 / np.sqrt(K) * fk[:, None], "e5m2")
    return {
        "xt_words": xtp[0],
        "xt_scales": xtp[1],
        "xo_words": xop[0],
        "xo_scales": xop[1],
        "w_words": wp[0],
        "w_scales": wp[1],
        "w0_words": w0p[0],
        "w0_scales": w0p[1],
        "xc_words": xcp[0],
        "xc_scales": xcp[1],
        "wg_words": wgp[0],
        "wg_scales": wgp[1],
        "wb_words": wbp[0],
        "wb_scales": wbp[1],
        "ws_words": wsp[0],
        "ws_scales": wsp[1],
        "so": (np.random.uniform(0.5, 1.6, (N, 1))).astype(np.float32),
        "sp": (np.random.uniform(0.5, 1.6, (N, 1))).astype(np.float32),
        "offs": striped(idx),
        "offs2": striped(idx2),
        "offs3": striped8(idx3),
        "offs4": striped8(idx4),
        "offs5": striped(idx5),
        "offs6": striped(idx6),
        "offs7": striped(idx7),
    }


def reference(xt_words, xt_scales, xo_words, xo_scales, w_words, w_scales, w0_words, w0_scales, xc_words, xc_scales, wg_words, wg_scales, wb_words, wb_scales, ws_words, ws_scales, so, sp, offs, offs2, offs3, offs4, offs5, offs6, offs7):
    idx = unstriped(offs)
    idx2 = unstriped(offs2)
    idx3 = unstriped8(offs3)
    idx4 = unstriped8(offs4)
    idx5 = unstriped(offs5)
    idx6 = unstriped(offs6)
    idx7 = unstriped(offs7)
    xtu = unpack_weight(xt_words, xt_scales, "e4m3")
    xou = unpack_weight(xo_words, xo_scales, "e2m1")
    wu = unpack_weight(w_words, w_scales, "e2m1")
    w0u = unpack_weight(w0_words, w0_scales, "e5m2")
    xcu = unpack_weight(xc_words, xc_scales, "e4m3")
    wgu = unpack_weight(wg_words, wg_scales, "e2m1")
    wbu = unpack_weight(wb_words, wb_scales, "e5m2")
    wsu = unpack_weight(ws_words, ws_scales, "e5m2")
    xtidxg = xtu[:, idx]
    xoidx2g = xou[:, idx2]
    a = wu.T @ xtidxg + w0u.T @ xoidx2g
    g0 = wgu.T @ xcu
    ga = g0[:, 0:1]
    gb = g0[:, 64:65]
    h1 = np.maximum(pick8(a, idx3, 64) * ga, pick8(a, idx4, 64) * gb)
    hid = np.concatenate([h1, g0], axis=1)
    hidq = mxq(hid, 0, "e4m3")
    xtidx5g = xtu[:, idx5]
    p = wbu.T @ hidq + wsu.T @ xtidx5g
    y = np.maximum(p[:, idx6] * f64(so), p[:, idx7] * f64(sp))
    return y

@@ -1,0 +1,222 @@
+from contextlib import ExitStack
+
+import concourse.mybir as mybir
+
+K, T, J, R, F, Z, M, Q, O, D, N, U = 512, 1024, 256, 512, 512, 1024, 512, 128, 128, 256, 256, 128
+FLOPS = 2 * (K * R * J + F * R * J + M * R * Q + R * N * D + K * N * D)
+
+F32 = mybir.dt.float32
+BF16 = mybir.dt.bfloat16
+I32 = mybir.dt.int32
+U32 = mybir.dt.uint32
+U16 = mybir.dt.uint16
+U8 = mybir.dt.uint8
+E4M3 = mybir.dt.float8_e4m3fn_x4
+E5M2 = mybir.dt.float8_e5m2_x4
+E2M1 = mybir.dt.float4_e2m1fn_x4
+COPY = mybir.ActivationFunctionType.Copy
+MAX = mybir.AluOpType.max
+
+P = 128
+PACK = 4
+QUADS = 4
+QUAD = 32
+LIVE = 4
+
+
+def tile_list_ctxgroups_bank_further_pairweighed_kernel(
+    tc, xt_words, xt_scales, xo_words, xo_scales, w_words, w_scales, w0_words, w0_scales,
+    xc_words, xc_scales, wg_words, wg_scales, wb_words, wb_scales, ws_words, ws_scales,
+    so, sp, offs, offs2, offs3, offs4, offs5, offs6, offs7, out,
+):
+    nc = tc.nc
+    with ExitStack() as ctx:
+        sb = ctx.enter_context(tc.tile_pool(name="sb", bufs=1))
+        ps = ctx.enter_context(tc.psum_pool(name="ps", bufs=1))
+
+        def tile(name, shape, dtype, tag=None):
+            return sb.tile(shape, dtype, name=name, tag=tag or name, align_bytes=64)
+
+        def load_list(name, src):
+            lst = tile(name, list(src.shape), U16)
+            nc.sync.dma_start(lst[:], src)
+            return lst
+
+        def load_words(name, src, cols, dtype, queue=nc.sync):
+            words = tile(name, [P, cols], dtype)
+            flat = src[0] if len(src.shape) == 3 else src[0].rearrange("p c r -> p (c r)")
+            queue.dma_start(words[:].bitcast(I32), flat.bitcast(I32))
+            return words
+
+        xt_stage = tile("xt_stage", [LIVE, QUADS, T // 4], I32)
+        raw_stage = tile("raw_stage", [LIVE, QUADS, (3 * R + Q) // 4], I32)
+        xt_plane = tile("xt_plane", [P, T], U8)
+        xo_plane = tile("xo_plane", [P, Z], U8)
+        raw_plane = tile("raw_plane", [P, 3 * R + Q], U8)
+        out_plane = tile("out_plane", [P, 2 * N], U8)
+        for plane in (xo_plane, raw_plane, xt_plane, out_plane):
+            nc.vector.memset(plane[:].bitcast(I32), 0)
+
+        def stage_rows(dst, src):
+            nc.sync.dma_start(dst, src[0].bitcast(I32).rearrange("(q r) c -> r q c", r=LIVE))
+
+        def place_rows(plane, cols, src, q):
+            nc.sync.dma_start(
+                plane[QUAD * q:QUAD * q + LIVE, cols].bitcast(I32), src[0].bitcast(I32)[LIVE * q:LIVE * (q + 1), :]
+            )
+
+        col = 0
+        for src in (w_scales, w0_scales, wg_scales, xc_scales):
+            width = src.shape[2] // 4
+            stage_rows(raw_stage[:, :, col:col + width], src)
+            col = col + width
+        stage_rows(xt_stage[:], xt_scales)
+        wg_sb = load_words("wg_sb", wg_words, R, U16)
+        xc_sb = load_words("xc_sb", xc_words, Q, U32)
+        xt_sb = load_words("xt_sb", xt_words, T, U32)
+        l1 = load_list("l1", offs)
+        w_sb = load_words("w_sb", w_words, R, U16)
+        w0_sb = load_words("w0_sb", w0_words, R, U32)
+        l2 = load_list("l2", offs2)
+        place_rows(xo_plane, slice(0, Z), xo_scales, 0)
+        xo_sb = load_words("xo_sb", xo_words, Z, U16)
+        for q in (2, 1, 3):
+            place_rows(xo_plane, slice(0, Z), xo_scales, q)
+        l5 = load_list("l5", offs5)
+        l3 = load_list("l3", offs3)
+        l4 = load_list("l4", offs4)
+        ws_sb = load_words("ws_sb", ws_words, N, U32)
+        wb_sb = load_words("wb_sb", wb_words, N, U32)
+        for i, src in enumerate((ws_scales, wb_scales)):
+            for q in range(QUADS):
+                nc.sync.dma_start(
+                    out_plane[QUAD * q:QUAD * q + LIVE, i * N:(i + 1) * N].bitcast(I32),
+                    src[0].bitcast(I32)[LIVE * q:LIVE * (q + 1), :],
+                )
+        l6 = load_list("l6", offs6)
+        l7 = load_list("l7", offs7)
+        so_sb = tile("so_sb", [P, 2], F32)
+        sp_sb = tile("sp_sb", [P, 2], F32)
+        with nc.allow_non_contiguous_dma(reason="one weight a partition and half"):
+            nc.sync.dma_start(so_sb[:], so.rearrange("(h p) o -> p (h o)", p=P))
+            nc.sync.dma_start(sp_sb[:], sp.rearrange("(h p) o -> p (h o)", p=P))
+
+        def gather(name, window, lst, dtype):
+            got = tile(name, [P, 16 * lst.shape[1]], dtype)
+            nc.vector.tensor_copy(got[:], window[:].indirect(lst[:]))
+            return got
+
+        def spread(plane, stage, quads):
+            for q in quads:
+                nc.vector.tensor_copy(plane[QUAD * q:QUAD * q + LIVE, :].bitcast(I32), stage[:, q, :])
+
+        w_dealt = tile("w_dealt", [P, PACK, P], U16)
+        wg_dealt = tile("wg_dealt", [P, PACK, P], U16)
+        w0_dealt = tile("w0_dealt", [P, PACK, P], U32)
+        nc.scalar.copy(wg_dealt[:], wg_sb[:].rearrange("p (m t) -> p t m", t=PACK))
+        nc.scalar.copy(w_dealt[:], w_sb[:].rearrange("p (m t) -> p t m", t=PACK))
+        nc.scalar.copy(
+            w0_dealt[:].rearrange("p t (b i) -> p b t i", i=4),
+            w0_sb[:].rearrange("p (b i t) -> p b t i", i=4, t=PACK),
+        )
+
+        spread(raw_plane, raw_stage, range(QUADS))
+        dealt_plane = [tile("dealt_plane%d" % x, [P, PACK, P], U8) for x in range(3)]
+        for x in (2, 0, 1):
+            nc.gpsimd.tensor_copy(dealt_plane[x][:], raw_plane[:, x * R:(x + 1) * R].rearrange("p (m t) -> p t m", t=PACK))
+        spread(xt_plane, xt_stage, reversed(range(QUADS)))
+        xt1_plane = gather("xt1_plane", xt_plane, l1, U8)
+        xt1 = gather("xt1", xt_sb, l1, U32)
+        xo2 = gather("xo2", xo_sb, l2, U16)
+        xo2_plane = gather("xo2_plane", xo_plane, l2, U8)
+
+        g_ps = ps.tile([P, PACK, Q], F32, name="g_ps")
+        a_ps = [ps.tile([P, J], F32, name="a_ps%d" % t, tag="bank%d" % t) for t in range(PACK)]
+
+        def tokens_pass(t):
+            nc.tensor.matmul_mx(
+                out=a_ps[t][:], lhsT=w_dealt[:, t, :].bitcast(E2M1), lhsT_scale=dealt_plane[0][:, t, :],
+                rhs=xt1[:].bitcast(E4M3), rhs_scale=xt1_plane[:], start=True, stop=False,
+            )
+
+        def notes_pass(t):
+            nc.tensor.matmul_mx(
+                out=a_ps[t][:], lhsT=w0_dealt[:, t, :].bitcast(E5M2), lhsT_scale=dealt_plane[1][:, t, :],
+                rhs=xo2[:].bitcast(E2M1), rhs_scale=xo2_plane[:], start=False, stop=True,
+            )
+
+        for t in range(PACK):
+            nc.tensor.matmul_mx(
+                out=g_ps[:, t, :], lhsT=wg_dealt[:, t, :].bitcast(E2M1), lhsT_scale=dealt_plane[2][:, t, :],
+                rhs=xc_sb[:].bitcast(E4M3), rhs_scale=raw_plane[:, 3 * R:3 * R + Q], start=True, stop=True,
+            )
+        for t in range(PACK):
+            tokens_pass(t)
+            notes_pass(t)
+        gains = tile("gains", [P, PACK, 2], F32)
+        nc.scalar.copy(gains[:], g_ps[:, :, 0:Q:64])
+        hid_g = tile("hid_g", [P, Q, PACK], BF16, tag="w0_sb")
+        nc.scalar.copy(hid_g[:], g_ps[:].rearrange("p t q -> p q t"))
+
+        xt5 = gather("xt5", xt_sb, l5, U32)
+        xt5_plane = gather("xt5_plane", xt_plane, l5, U8)
+
+        a_sb = [tile("a_sb%d" % t, [P, J], F32) for t in range(PACK)]
+        first = tile("first", [P, PACK, O], F32)
+        second = tile("second", [P, PACK, O], F32)
+        hid_h = tile("hid_h", [P, O, PACK], BF16)
+        nc.scalar.copy(a_sb[0][:], a_ps[0][:])
+        for t in range(1, PACK):
+            nc.vector.tensor_copy(a_sb[t][:], a_ps[t][:])
+
+        def quantise(name, hid, tag=None):
+            codes = tile(name + "_codes", [P, P], U32, tag=tag)
+            plane = tile(name + "_plane", [P, P], U8)
+            nc.vector.quantize_mx(out=codes[:].bitcast(E4M3), scales=plane[:], in_=hid[:].rearrange("p d t -> p (d t)"))
+            return codes, plane
+
+        hq_g, hq_g_plane = quantise("hq_g", hid_g, tag="w0_dealt")
+
+        def short_way(acc, h, cols, start, stop):
+            nc.tensor.matmul_mx(
+                out=acc, lhsT=ws_sb[:, h * P:(h + 1) * P].bitcast(E5M2), lhsT_scale=out_plane[:, h * P:(h + 1) * P],
+                rhs=xt5[:, cols].bitcast(E4M3), rhs_scale=xt5_plane[:, cols], start=start, stop=stop,
+            )
+
+        def output_matrix(acc, h, codes, plane, start, stop):
+            nc.tensor.matmul_mx(
+                out=acc, lhsT=wb_sb[:, h * P:(h + 1) * P].bitcast(E5M2), lhsT_scale=out_plane[:, N + h * P:N + (h + 1) * P],
+                rhs=codes[:].bitcast(E4M3), rhs_scale=plane[:], start=start, stop=stop,
+            )
+
+        pg_ps = ps.tile([P, 2, Q], F32, name="pg_ps", tag="bank2")
+        ph_ps = [ps.tile([P, O], F32, name="ph_ps%d" % h, tag="bank%d" % h) for h in range(2)]
+        for h in range(2):
+            short_way(pg_ps[:, h, :], h, slice(O, D), True, False)
+            output_matrix(pg_ps[:, h, :], h, hq_g, hq_g_plane, False, True)
+        for h in range(2):
+            short_way(ph_ps[h][:], h, slice(0, O), True, False)
+        p_sb = [tile("p_sb%d" % h, [P, D], F32) for h in range(2)]
+
+        for t in range(PACK):
+            nc.scalar.activation(first[:, t, :], a_sb[t][:].indirect(l3[:]), COPY, scale=gains[:, t, 0:1])
+            nc.scalar.activation(second[:, t, :], a_sb[t][:].indirect(l4[:]), COPY, scale=gains[:, t, 1:2])
+        nc.vector.tensor_tensor(
+            hid_h[:].rearrange("p (b i) t -> p b t i", i=4), first[:].rearrange("p t (b i) -> p b t i", i=4),
+            second[:].rearrange("p t (b i) -> p b t i", i=4), MAX,
+        )
+        for h in range(2):
+            nc.scalar.copy(p_sb[h][:, O:D], pg_ps[:, h, :])
+        hq_h, hq_h_plane = quantise("hq_h", hid_h)
+        for h in range(2):
+            output_matrix(ph_ps[h][:], h, hq_h, hq_h_plane, False, True)
+        for h in range(2):
+            nc.vector.tensor_copy(p_sb[h][:, 0:O], ph_ps[h][:])
+        for h in range(2):
+            y6 = tile("y6_%d" % h, [P, U], F32)
+            y7 = tile("y7_%d" % h, [P, U], F32)
+            y = tile("y_%d" % h, [P, U], F32)
+            nc.scalar.activation(y6[:], p_sb[h][:].indirect(l6[:]), COPY, scale=so_sb[:, h:h + 1])
+            nc.scalar.activation(y7[:], p_sb[h][:].indirect(l7[:]), COPY, scale=sp_sb[:, h:h + 1])
+            nc.vector.tensor_tensor(y[:], y6[:], y7[:], MAX)
+            nc.sync.dma_start(out[h * P:(h + 1) * P, :], y[:])

@@ -48,13 +48,12 @@ def tile_list_ctxgroups_bank_further_pairweighed_kernel(
             queue.dma_start(words[:].bitcast(I32), flat.bitcast(I32))
             return words
 
-        xt_stage = tile("xt_stage", [LIVE, QUADS, T // 4], I32)
         raw_stage = tile("raw_stage", [LIVE, QUADS, (3 * R + Q) // 4], I32)
         xt_plane = tile("xt_plane", [P, T], U8)
         xo_plane = tile("xo_plane", [P, Z], U8)
         raw_plane = tile("raw_plane", [P, 3 * R + Q], U8)
         out_plane = tile("out_plane", [P, 2 * N], U8)
-        for plane in (xo_plane, raw_plane, xt_plane, out_plane):
+        for plane in (xt_plane, xo_plane, raw_plane, out_plane):
             nc.vector.memset(plane[:].bitcast(I32), 0)
 
         def stage_rows(dst, src):
@@ -70,21 +69,21 @@ def tile_list_ctxgroups_bank_further_pairweighed_kernel(
             width = src.shape[2] // 4
             stage_rows(raw_stage[:, :, col:col + width], src)
             col = col + width
-        stage_rows(xt_stage[:], xt_scales)
-        wg_sb = load_words("wg_sb", wg_words, R, U16)
-        xc_sb = load_words("xc_sb", xc_words, Q, U32)
-        xt_sb = load_words("xt_sb", xt_words, T, U32)
         l1 = load_list("l1", offs)
+        xc_sb = load_words("xc_sb", xc_words, Q, U32)
+        wg_sb = load_words("wg_sb", wg_words, R, U16)
+        xt_sb = load_words("xt_sb", xt_words, T, U32)
+        for q in (0, 2, 1, 3):
+            place_rows(xt_plane, slice(0, T), xt_scales, q)
         w_sb = load_words("w_sb", w_words, R, U16)
+        xo_sb = load_words("xo_sb", xo_words, Z, U16)
         w0_sb = load_words("w0_sb", w0_words, R, U32)
         l2 = load_list("l2", offs2)
-        place_rows(xo_plane, slice(0, Z), xo_scales, 0)
-        xo_sb = load_words("xo_sb", xo_words, Z, U16)
-        for q in (2, 1, 3):
+        for q in (0, 2, 1, 3):
             place_rows(xo_plane, slice(0, Z), xo_scales, q)
-        l5 = load_list("l5", offs5)
-        l3 = load_list("l3", offs3)
         l4 = load_list("l4", offs4)
+        l3 = load_list("l3", offs3)
+        l5 = load_list("l5", offs5)
         ws_sb = load_words("ws_sb", ws_words, N, U32)
         wb_sb = load_words("wb_sb", wb_words, N, U32)
         for i, src in enumerate((ws_scales, wb_scales)):
@@ -121,53 +120,62 @@ def tile_list_ctxgroups_bank_further_pairweighed_kernel(
         )
 
         spread(raw_plane, raw_stage, range(QUADS))
-        dealt_plane = [tile("dealt_plane%d" % x, [P, PACK, P], U8) for x in range(3)]
-        for x in (2, 0, 1):
-            nc.gpsimd.tensor_copy(dealt_plane[x][:], raw_plane[:, x * R:(x + 1) * R].rearrange("p (m t) -> p t m", t=PACK))
-        spread(xt_plane, xt_stage, reversed(range(QUADS)))
-        xt1_plane = gather("xt1_plane", xt_plane, l1, U8)
+        def by_t(x):
+            return raw_plane[:, x * R:(x + 1) * R].rearrange("p (m t) -> p t m", t=PACK)
+
+        wg_plane = tile("wg_plane", [P, PACK, P], U8)
+        w_plane = tile("w_plane", [P, PACK, P], U8)
+        w0_head = tile("w0_head", [P, 2, P], U8)
+        nc.vector.tensor_copy(wg_plane[:], by_t(2))
+        nc.vector.tensor_copy(w_plane[:], by_t(0))
+        nc.vector.tensor_copy(w0_head[:], by_t(1)[:, 0:2, :])
         xt1 = gather("xt1", xt_sb, l1, U32)
+        xt1_plane = gather("xt1_plane", xt_plane, l1, U8)
         xo2 = gather("xo2", xo_sb, l2, U16)
-        xo2_plane = gather("xo2_plane", xo_plane, l2, U8)
+        xo2_plane = tile("xo2_plane", [P, J], U8)
+        for half in range(2):
+            nc.vector.tensor_copy(xo2_plane[:, half * P:(half + 1) * P], xo_plane[:].indirect(l2[:, 8 * half:8 * (half + 1)]))
+        w0_rest = tile("w0_rest", [P, 2, P], U8, tag="xo_plane")
+        nc.vector.tensor_copy(w0_rest[:], by_t(1)[:, 2:4, :])
+        w0_plane = [w0_head[:, 0, :], w0_head[:, 1, :], w0_rest[:, 0, :], w0_rest[:, 1, :]]
 
         g_ps = ps.tile([P, PACK, Q], F32, name="g_ps")
-        a_ps = [ps.tile([P, J], F32, name="a_ps%d" % t, tag="bank%d" % t) for t in range(PACK)]
-
-        def tokens_pass(t):
-            nc.tensor.matmul_mx(
-                out=a_ps[t][:], lhsT=w_dealt[:, t, :].bitcast(E2M1), lhsT_scale=dealt_plane[0][:, t, :],
-                rhs=xt1[:].bitcast(E4M3), rhs_scale=xt1_plane[:], start=True, stop=False,
-            )
-
-        def notes_pass(t):
-            nc.tensor.matmul_mx(
-                out=a_ps[t][:], lhsT=w0_dealt[:, t, :].bitcast(E5M2), lhsT_scale=dealt_plane[1][:, t, :],
-                rhs=xo2[:].bitcast(E2M1), rhs_scale=xo2_plane[:], start=False, stop=True,
-            )
+        pieces = [(0, slice(0, P)), (0, slice(P, J))] + [(t, slice(0, J)) for t in range(1, PACK)]
+        a_ps = [
+            ps.tile([P, cols.stop - cols.start], F32, name="a_ps%d" % i, tag="bank%d" % i) for i, (t, cols) in enumerate(pieces)
+        ]
 
         for t in range(PACK):
             nc.tensor.matmul_mx(
-                out=g_ps[:, t, :], lhsT=wg_dealt[:, t, :].bitcast(E2M1), lhsT_scale=dealt_plane[2][:, t, :],
+                out=g_ps[:, t, :], lhsT=wg_dealt[:, t, :].bitcast(E2M1), lhsT_scale=wg_plane[:, t, :],
                 rhs=xc_sb[:].bitcast(E4M3), rhs_scale=raw_plane[:, 3 * R:3 * R + Q], start=True, stop=True,
             )
-        for t in range(PACK):
-            tokens_pass(t)
-            notes_pass(t)
+        for i, (t, cols) in enumerate(pieces):
+            nc.tensor.matmul_mx(
+                out=a_ps[i][:], lhsT=w_dealt[:, t, :].bitcast(E2M1), lhsT_scale=w_plane[:, t, :],
+                rhs=xt1[:, cols].bitcast(E4M3), rhs_scale=xt1_plane[:, cols], start=True, stop=False,
+            )
+            nc.tensor.matmul_mx(
+                out=a_ps[i][:], lhsT=w0_dealt[:, t, :].bitcast(E5M2), lhsT_scale=w0_plane[t],
+                rhs=xo2[:, cols].bitcast(E2M1), rhs_scale=xo2_plane[:, cols], start=False, stop=True,
+            )
         gains = tile("gains", [P, PACK, 2], F32)
         nc.scalar.copy(gains[:], g_ps[:, :, 0:Q:64])
         hid_g = tile("hid_g", [P, Q, PACK], BF16, tag="w0_sb")
         nc.scalar.copy(hid_g[:], g_ps[:].rearrange("p t q -> p q t"))
 
-        xt5 = gather("xt5", xt_sb, l5, U32)
-        xt5_plane = gather("xt5_plane", xt_plane, l5, U8)
-
         a_sb = [tile("a_sb%d" % t, [P, J], F32) for t in range(PACK)]
         first = tile("first", [P, PACK, O], F32)
         second = tile("second", [P, PACK, O], F32)
         hid_h = tile("hid_h", [P, O, PACK], BF16)
-        nc.scalar.copy(a_sb[0][:], a_ps[0][:])
-        for t in range(1, PACK):
-            nc.vector.tensor_copy(a_sb[t][:], a_ps[t][:])
+        for i, (t, cols) in enumerate(pieces):
+            if t == 0:
+                nc.scalar.copy(a_sb[t][:, cols], a_ps[i][:])
+            else:
+                nc.vector.tensor_copy(a_sb[t][:, cols], a_ps[i][:])
+
+        xt5 = gather("xt5", xt_sb, l5, U32)
+        xt5_plane = gather("xt5_plane", xt_plane, l5, U8)
 
         def quantise(name, hid, tag=None):
             codes = tile(name + "_codes", [P, P], U32, tag=tag)
@@ -189,7 +197,7 @@ def tile_list_ctxgroups_bank_further_pairweighed_kernel(
                 rhs=codes[:].bitcast(E4M3), rhs_scale=plane[:], start=start, stop=stop,
             )
 
-        pg_ps = ps.tile([P, 2, Q], F32, name="pg_ps", tag="bank2")
+        pg_ps = ps.tile([P, 2, Q], F32, name="pg_ps", tag="bank3")
         ph_ps = [ps.tile([P, O], F32, name="ph_ps%d" % h, tag="bank%d" % h) for h in range(2)]
         for h in range(2):
             short_way(pg_ps[:, h, :], h, slice(O, D), True, False)
@@ -198,16 +206,27 @@ def tile_list_ctxgroups_bank_further_pairweighed_kernel(
             short_way(ph_ps[h][:], h, slice(0, O), True, False)
         p_sb = [tile("p_sb%d" % h, [P, D], F32) for h in range(2)]
 
-        for t in range(PACK):
-            nc.scalar.activation(first[:, t, :], a_sb[t][:].indirect(l3[:]), COPY, scale=gains[:, t, 0:1])
-            nc.scalar.activation(second[:, t, :], a_sb[t][:].indirect(l4[:]), COPY, scale=gains[:, t, 1:2])
-        nc.vector.tensor_tensor(
-            hid_h[:].rearrange("p (b i) t -> p b t i", i=4), first[:].rearrange("p t (b i) -> p b t i", i=4),
-            second[:].rearrange("p t (b i) -> p b t i", i=4), MAX,
-        )
+        def look(t, cols):
+            entries = slice(cols.start // 16, cols.stop // 16)
+            nc.scalar.activation(first[:, t, cols], a_sb[t][:].indirect(l3[:, entries]), COPY, scale=gains[:, t, 0:1])
+            nc.scalar.activation(second[:, t, cols], a_sb[t][:].indirect(l4[:, entries]), COPY, scale=gains[:, t, 1:2])
+
+        for t in range(PACK - 1):
+            look(t, slice(0, O))
+        hq_h = tile("hq_h_codes", [P, O], U32)
+        hq_h_plane = tile("hq_h_plane", [P, O], U8)
+        halves = (slice(0, O // 2), slice(O // 2, O))
+        for cols in halves:
+            look(PACK - 1, cols)
+            nc.vector.tensor_tensor(
+                hid_h[:, cols, :].rearrange("p (b i) t -> p b t i", i=4), first[:, :, cols].rearrange("p t (b i) -> p b t i", i=4),
+                second[:, :, cols].rearrange("p t (b i) -> p b t i", i=4), MAX,
+            )
+            nc.vector.quantize_mx(
+                out=hq_h[:, cols].bitcast(E4M3), scales=hq_h_plane[:, cols], in_=hid_h[:, cols, :].rearrange("p d t -> p (d t)")
+            )
         for h in range(2):
             nc.scalar.copy(p_sb[h][:, O:D], pg_ps[:, h, :])
-        hq_h, hq_h_plane = quantise("hq_h", hid_h)
         for h in range(2):
             output_matrix(ph_ps[h][:], h, hq_h, hq_h_plane, False, True)
         for h in range(2):

@@ -124,20 +124,20 @@ def tile_list_ctxgroups_bank_further_pairweighed_kernel(
             return raw_plane[:, x * R:(x + 1) * R].rearrange("p (m t) -> p t m", t=PACK)
 
         wg_plane = tile("wg_plane", [P, PACK, P], U8)
-        w_plane = tile("w_plane", [P, PACK, P], U8)
-        w0_head = tile("w0_head", [P, 2, P], U8)
+        head_plane = tile("head_plane", [P, 2, 2, P], U8)
+        both = raw_plane[:, 0:2 * R].rearrange("p (x m t) -> p x t m", x=2, t=PACK)
         nc.vector.tensor_copy(wg_plane[:], by_t(2))
-        nc.vector.tensor_copy(w_plane[:], by_t(0))
-        nc.vector.tensor_copy(w0_head[:], by_t(1)[:, 0:2, :])
+        nc.vector.tensor_copy(head_plane[:], both[:, :, 0:2, :])
         xt1 = gather("xt1", xt_sb, l1, U32)
         xt1_plane = gather("xt1_plane", xt_plane, l1, U8)
         xo2 = gather("xo2", xo_sb, l2, U16)
         xo2_plane = tile("xo2_plane", [P, J], U8)
         for half in range(2):
             nc.vector.tensor_copy(xo2_plane[:, half * P:(half + 1) * P], xo_plane[:].indirect(l2[:, 8 * half:8 * (half + 1)]))
-        w0_rest = tile("w0_rest", [P, 2, P], U8, tag="xo_plane")
-        nc.vector.tensor_copy(w0_rest[:], by_t(1)[:, 2:4, :])
-        w0_plane = [w0_head[:, 0, :], w0_head[:, 1, :], w0_rest[:, 0, :], w0_rest[:, 1, :]]
+        rest_plane = tile("rest_plane", [P, 2, 2, P], U8, tag="xo_plane")
+        nc.vector.tensor_copy(rest_plane[:], both[:, :, 2:4, :])
+        w_plane = [(head_plane, rest_plane)[t // 2][:, 0, t % 2, :] for t in range(PACK)]
+        w0_plane = [(head_plane, rest_plane)[t // 2][:, 1, t % 2, :] for t in range(PACK)]
 
         g_ps = ps.tile([P, PACK, Q], F32, name="g_ps")
         pieces = [(0, slice(0, P)), (0, slice(P, J))] + [(t, slice(0, J)) for t in range(1, PACK)]
@@ -152,14 +152,14 @@ def tile_list_ctxgroups_bank_further_pairweighed_kernel(
             )
         for i, (t, cols) in enumerate(pieces):
             nc.tensor.matmul_mx(
-                out=a_ps[i][:], lhsT=w_dealt[:, t, :].bitcast(E2M1), lhsT_scale=w_plane[:, t, :],
+                out=a_ps[i][:], lhsT=w_dealt[:, t, :].bitcast(E2M1), lhsT_scale=w_plane[t],
                 rhs=xt1[:, cols].bitcast(E4M3), rhs_scale=xt1_plane[:, cols], start=True, stop=False,
             )
             nc.tensor.matmul_mx(
                 out=a_ps[i][:], lhsT=w0_dealt[:, t, :].bitcast(E5M2), lhsT_scale=w0_plane[t],
                 rhs=xo2[:, cols].bitcast(E2M1), rhs_scale=xo2_plane[:, cols], start=False, stop=True,
             )
-        gains = tile("gains", [P, PACK, 2], F32)
+        gains = tile("gains", [P, PACK, 2], F32, tag="w_sb")
         nc.scalar.copy(gains[:], g_ps[:, :, 0:Q:64])
         hid_g = tile("hid_g", [P, Q, PACK], BF16, tag="w0_sb")
         nc.scalar.copy(hid_g[:], g_ps[:].rearrange("p t q -> p q t"))

from contextlib import ExitStack

import concourse.mybir as mybir

K, T, J, R, F, Z, M, Q, O, D, N, U = 512, 1024, 256, 512, 512, 1024, 512, 128, 128, 256, 256, 128
FLOPS = 2 * (K * R * J + F * R * J + M * R * Q + R * N * D + K * N * D)

F32 = mybir.dt.float32
BF16 = mybir.dt.bfloat16
I32 = mybir.dt.int32
U32 = mybir.dt.uint32
U16 = mybir.dt.uint16
U8 = mybir.dt.uint8
E4M3 = mybir.dt.float8_e4m3fn_x4
E5M2 = mybir.dt.float8_e5m2_x4
E2M1 = mybir.dt.float4_e2m1fn_x4
COPY = mybir.ActivationFunctionType.Copy
MAX = mybir.AluOpType.max

P = 128
PACK = 4
QUADS = 4
QUAD = 32
LIVE = 4


def tile_list_ctxgroups_bank_further_pairweighed_kernel(
    tc, xt_words, xt_scales, xo_words, xo_scales, w_words, w_scales, w0_words, w0_scales,
    xc_words, xc_scales, wg_words, wg_scales, wb_words, wb_scales, ws_words, ws_scales,
    so, sp, offs, offs2, offs3, offs4, offs5, offs6, offs7, out,
):
    nc = tc.nc
    with ExitStack() as ctx:
        sb = ctx.enter_context(tc.tile_pool(name="sb", bufs=1))
        ps = ctx.enter_context(tc.psum_pool(name="ps", bufs=1))

        def tile(name, shape, dtype, tag=None):
            return sb.tile(shape, dtype, name=name, tag=tag or name, align_bytes=64)

        def load_list(name, src):
            lst = tile(name, list(src.shape), U16)
            nc.sync.dma_start(lst[:], src)
            return lst

        def load_words(name, src, cols, dtype, queue=nc.sync):
            words = tile(name, [P, cols], dtype)
            flat = src[0] if len(src.shape) == 3 else src[0].rearrange("p c r -> p (c r)")
            queue.dma_start(words[:].bitcast(I32), flat.bitcast(I32))
            return words

        raw_stage = tile("raw_stage", [LIVE, QUADS, (3 * R + Q) // 4], I32)
        xt_plane = tile("xt_plane", [P, T], U8)
        xo_plane = tile("xo_plane", [P, Z], U8)
        raw_plane = tile("raw_plane", [P, 3 * R + Q], U8)
        out_plane = tile("out_plane", [P, 2 * N], U8)
        for plane in (xt_plane, xo_plane, raw_plane, out_plane):
            nc.vector.memset(plane[:].bitcast(I32), 0)

        def stage_rows(dst, src):
            nc.sync.dma_start(dst, src[0].bitcast(I32).rearrange("(q r) c -> r q c", r=LIVE))

        def place_rows(plane, cols, src, q):
            nc.sync.dma_start(
                plane[QUAD * q:QUAD * q + LIVE, cols].bitcast(I32), src[0].bitcast(I32)[LIVE * q:LIVE * (q + 1), :]
            )

        col = 0
        for src in (w_scales, w0_scales, wg_scales, xc_scales):
            width = src.shape[2] // 4
            stage_rows(raw_stage[:, :, col:col + width], src)
            col = col + width
        l1 = load_list("l1", offs)
        xc_sb = load_words("xc_sb", xc_words, Q, U32)
        wg_sb = load_words("wg_sb", wg_words, R, U16)
        xt_sb = load_words("xt_sb", xt_words, T, U32)
        for q in (0, 2, 1, 3):
            place_rows(xt_plane, slice(0, T), xt_scales, q)
        w_sb = load_words("w_sb", w_words, R, U16)
        xo_sb = load_words("xo_sb", xo_words, Z, U16)
        w0_sb = load_words("w0_sb", w0_words, R, U32)
        l2 = load_list("l2", offs2)
        for q in (0, 2, 1, 3):
            place_rows(xo_plane, slice(0, Z), xo_scales, q)
        l4 = load_list("l4", offs4)
        l3 = load_list("l3", offs3)
        l5 = load_list("l5", offs5)
        ws_sb = load_words("ws_sb", ws_words, N, U32)
        wb_sb = load_words("wb_sb", wb_words, N, U32)
        for i, src in enumerate((ws_scales, wb_scales)):
            for q in range(QUADS):
                nc.sync.dma_start(
                    out_plane[QUAD * q:QUAD * q + LIVE, i * N:(i + 1) * N].bitcast(I32),
                    src[0].bitcast(I32)[LIVE * q:LIVE * (q + 1), :],
                )
        l6 = load_list("l6", offs6)
        l7 = load_list("l7", offs7)
        so_sb = tile("so_sb", [P, 2], F32)
        sp_sb = tile("sp_sb", [P, 2], F32)
        with nc.allow_non_contiguous_dma(reason="one weight a partition and half"):
            nc.sync.dma_start(so_sb[:], so.rearrange("(h p) o -> p (h o)", p=P))
            nc.sync.dma_start(sp_sb[:], sp.rearrange("(h p) o -> p (h o)", p=P))

        def gather(name, window, lst, dtype):
            got = tile(name, [P, 16 * lst.shape[1]], dtype)
            nc.vector.tensor_copy(got[:], window[:].indirect(lst[:]))
            return got

        def spread(plane, stage, quads):
            for q in quads:
                nc.vector.tensor_copy(plane[QUAD * q:QUAD * q + LIVE, :].bitcast(I32), stage[:, q, :])

        w_dealt = tile("w_dealt", [P, PACK, P], U16)
        wg_dealt = tile("wg_dealt", [P, PACK, P], U16)
        w0_dealt = tile("w0_dealt", [P, PACK, P], U32)
        nc.scalar.copy(wg_dealt[:], wg_sb[:].rearrange("p (m t) -> p t m", t=PACK))
        nc.scalar.copy(w_dealt[:], w_sb[:].rearrange("p (m t) -> p t m", t=PACK))
        nc.scalar.copy(
            w0_dealt[:].rearrange("p t (b i) -> p b t i", i=4),
            w0_sb[:].rearrange("p (b i t) -> p b t i", i=4, t=PACK),
        )

        spread(raw_plane, raw_stage, range(QUADS))
        def by_t(x):
            return raw_plane[:, x * R:(x + 1) * R].rearrange("p (m t) -> p t m", t=PACK)

        wg_plane = tile("wg_plane", [P, PACK, P], U8)
        head_plane = tile("head_plane", [P, 2, 2, P], U8)
        both = raw_plane[:, 0:2 * R].rearrange("p (x m t) -> p x t m", x=2, t=PACK)
        nc.vector.tensor_copy(wg_plane[:], by_t(2))
        nc.vector.tensor_copy(head_plane[:], both[:, :, 0:2, :])
        xt1 = gather("xt1", xt_sb, l1, U32)
        xt1_plane = gather("xt1_plane", xt_plane, l1, U8)
        xo2 = gather("xo2", xo_sb, l2, U16)
        xo2_plane = tile("xo2_plane", [P, J], U8)
        for half in range(2):
            nc.vector.tensor_copy(xo2_plane[:, half * P:(half + 1) * P], xo_plane[:].indirect(l2[:, 8 * half:8 * (half + 1)]))
        rest_plane = tile("rest_plane", [P, 2, 2, P], U8, tag="xo_plane")
        nc.vector.tensor_copy(rest_plane[:], both[:, :, 2:4, :])
        w_plane = [(head_plane, rest_plane)[t // 2][:, 0, t % 2, :] for t in range(PACK)]
        w0_plane = [(head_plane, rest_plane)[t // 2][:, 1, t % 2, :] for t in range(PACK)]

        g_ps = ps.tile([P, PACK, Q], F32, name="g_ps")
        pieces = [(0, slice(0, P)), (0, slice(P, J))] + [(t, slice(0, J)) for t in range(1, PACK)]
        a_ps = [
            ps.tile([P, cols.stop - cols.start], F32, name="a_ps%d" % i, tag="bank%d" % i) for i, (t, cols) in enumerate(pieces)
        ]

        for t in range(PACK):
            nc.tensor.matmul_mx(
                out=g_ps[:, t, :], lhsT=wg_dealt[:, t, :].bitcast(E2M1), lhsT_scale=wg_plane[:, t, :],
                rhs=xc_sb[:].bitcast(E4M3), rhs_scale=raw_plane[:, 3 * R:3 * R + Q], start=True, stop=True,
            )
        for i, (t, cols) in enumerate(pieces):
            nc.tensor.matmul_mx(
                out=a_ps[i][:], lhsT=w_dealt[:, t, :].bitcast(E2M1), lhsT_scale=w_plane[t],
                rhs=xt1[:, cols].bitcast(E4M3), rhs_scale=xt1_plane[:, cols], start=True, stop=False,
            )
            nc.tensor.matmul_mx(
                out=a_ps[i][:], lhsT=w0_dealt[:, t, :].bitcast(E5M2), lhsT_scale=w0_plane[t],
                rhs=xo2[:, cols].bitcast(E2M1), rhs_scale=xo2_plane[:, cols], start=False, stop=True,
            )
        gains = tile("gains", [P, PACK, 2], F32, tag="w_sb")
        nc.scalar.copy(gains[:], g_ps[:, :, 0:Q:64])
        hid_g = tile("hid_g", [P, Q, PACK], BF16, tag="w0_sb")
        nc.scalar.copy(hid_g[:], g_ps[:].rearrange("p t q -> p q t"))

        a_sb = [tile("a_sb%d" % t, [P, J], F32) for t in range(PACK)]
        first = tile("first", [P, PACK, O], F32)
        second = tile("second", [P, PACK, O], F32)
        hid_h = tile("hid_h", [P, O, PACK], BF16)
        for i, (t, cols) in enumerate(pieces):
            if t == 0:
                nc.scalar.copy(a_sb[t][:, cols], a_ps[i][:])
            else:
                nc.vector.tensor_copy(a_sb[t][:, cols], a_ps[i][:])

        xt5 = gather("xt5", xt_sb, l5, U32)
        xt5_plane = gather("xt5_plane", xt_plane, l5, U8)

        def quantise(name, hid, tag=None):
            codes = tile(name + "_codes", [P, P], U32, tag=tag)
            plane = tile(name + "_plane", [P, P], U8)
            nc.vector.quantize_mx(out=codes[:].bitcast(E4M3), scales=plane[:], in_=hid[:].rearrange("p d t -> p (d t)"))
            return codes, plane

        hq_g, hq_g_plane = quantise("hq_g", hid_g, tag="w0_dealt")

        def short_way(acc, h, cols, start, stop):
            nc.tensor.matmul_mx(
                out=acc, lhsT=ws_sb[:, h * P:(h + 1) * P].bitcast(E5M2), lhsT_scale=out_plane[:, h * P:(h + 1) * P],
                rhs=xt5[:, cols].bitcast(E4M3), rhs_scale=xt5_plane[:, cols], start=start, stop=stop,
            )

        def output_matrix(acc, h, codes, plane, start, stop):
            nc.tensor.matmul_mx(
                out=acc, lhsT=wb_sb[:, h * P:(h + 1) * P].bitcast(E5M2), lhsT_scale=out_plane[:, N + h * P:N + (h + 1) * P],
                rhs=codes[:].bitcast(E4M3), rhs_scale=plane[:], start=start, stop=stop,
            )

        pg_ps = ps.tile([P, 2, Q], F32, name="pg_ps", tag="bank3")
        ph_ps = [ps.tile([P, O], F32, name="ph_ps%d" % h, tag="bank%d" % h) for h in range(2)]
        for h in range(2):
            short_way(pg_ps[:, h, :], h, slice(O, D), True, False)
            output_matrix(pg_ps[:, h, :], h, hq_g, hq_g_plane, False, True)
        for h in range(2):
            short_way(ph_ps[h][:], h, slice(0, O), True, False)
        p_sb = [tile("p_sb%d" % h, [P, D], F32) for h in range(2)]

        def look(t, cols):
            entries = slice(cols.start // 16, cols.stop // 16)
            nc.scalar.activation(first[:, t, cols], a_sb[t][:].indirect(l3[:, entries]), COPY, scale=gains[:, t, 0:1])
            nc.scalar.activation(second[:, t, cols], a_sb[t][:].indirect(l4[:, entries]), COPY, scale=gains[:, t, 1:2])

        for t in range(PACK - 1):
            look(t, slice(0, O))
        hq_h = tile("hq_h_codes", [P, O], U32)
        hq_h_plane = tile("hq_h_plane", [P, O], U8)
        halves = (slice(0, O // 2), slice(O // 2, O))
        for cols in halves:
            look(PACK - 1, cols)
            nc.vector.tensor_tensor(
                hid_h[:, cols, :].rearrange("p (b i) t -> p b t i", i=4), first[:, :, cols].rearrange("p t (b i) -> p b t i", i=4),
                second[:, :, cols].rearrange("p t (b i) -> p b t i", i=4), MAX,
            )
            nc.vector.quantize_mx(
                out=hq_h[:, cols].bitcast(E4M3), scales=hq_h_plane[:, cols], in_=hid_h[:, cols, :].rearrange("p d t -> p (d t)")
            )
        for h in range(2):
            nc.scalar.copy(p_sb[h][:, O:D], pg_ps[:, h, :])
        for h in range(2):
            output_matrix(ph_ps[h][:], h, hq_h, hq_h_plane, False, True)
        for h in range(2):
            nc.vector.tensor_copy(p_sb[h][:, 0:O], ph_ps[h][:])
        for h in range(2):
            y6 = tile("y6_%d" % h, [P, U], F32)
            y7 = tile("y7_%d" % h, [P, U], F32)
            y = tile("y_%d" % h, [P, U], F32)
            nc.scalar.activation(y6[:], p_sb[h][:].indirect(l6[:]), COPY, scale=so_sb[:, h:h + 1])
            nc.scalar.activation(y7[:], p_sb[h][:].indirect(l7[:]), COPY, scale=sp_sb[:, h:h + 1])
            nc.vector.tensor_tensor(y[:], y6[:], y7[:], MAX)
            nc.sync.dma_start(out[h * P:(h + 1) * P, :], y[:])
